import numpy as np
import ml_dtypes


def mxq(x, axis, fmt="e4m3"):
    dtype, down = {"e4m3": (ml_dtypes.float8_e4m3fn, 7), "e5m2": (ml_dtypes.float8_e5m2, 14)}[fmt]
    v = np.moveaxis(np.asarray(x, np.float32).astype(ml_dtypes.bfloat16).astype(np.float64), axis, -1)
    blocks = v.reshape(v.shape[:-1] + (-1, 32))
    amax = np.abs(blocks).max(-1, keepdims=True)
    byte = np.maximum(np.where(amax > 0, np.frexp(amax)[1] - 1 + 127, 0) - down, 1)
    scale = np.exp2(byte - 127.0)
    codes = (blocks / scale).astype(np.float32).astype(dtype).astype(np.float64)
    return np.moveaxis((codes * scale).reshape(v.shape), -1, axis)


WIDE = False


def mx_kscale(k):
    if not WIDE:
        return np.ones(k)
    levels = np.array([10, -10, 5, -5, 0])
    if k % 512:
        return np.exp2(np.random.permutation(np.resize(levels, k // 32))).repeat(32)
    a = np.empty((k // 512, 16))
    for p in range(k // 512):
        a[p, :8] = np.random.permutation(np.resize(levels, 8))
        for g in range(8):
            far = levels[np.abs(levels - a[p, g]) >= 10]
            a[p, g + 8] = far[np.random.randint(len(far))]
    return np.exp2(a.ravel()).repeat(32)


def f64(x):
    return np.asarray(x).astype(np.float64)


def striped8(idx):
    return np.asarray(idx).reshape(8, -1, 16).transpose(0, 2, 1).reshape(128, -1).astype(np.uint16)


def unstriped8(offs):
    return offs.reshape(8, 16, -1).transpose(0, 2, 1).reshape(8, -1).astype(np.int64)


def pick8(x, idx, run):
    r = np.arange(len(x))
    return x[r[:, None], idx[r % (8 * run) // run]]


E2M1 = np.array([0.0, 0.5, 1.0, 1.5, 2.0, 3.0, 4.0, 6.0, -0.0, -0.5, -1.0, -1.5, -2.0, -3.0, -4.0, -6.0])


def pack_weight(w, fmt):
    k, n = w.shape
    w = f64(np.asarray(w, np.float32).astype(ml_dtypes.bfloat16)).reshape(k // 32, 32, n)
    amax = np.abs(w).max(1)
    if fmt == "e4m3":
        byte = np.frexp(amax)[1] - 1 + 127 - 7
    else:
        mant, ex = np.frexp(amax / 6.0)
        byte = np.where(mant > 0.5, ex, ex - 1) + 127
    byte = np.clip(np.where(amax > 0, byte, 1), 1, 254)
    scaled = (w * np.exp2(127.0 - byte)[:, None, :]).reshape(k, n).astype(np.float32)
    by_word = np.ascontiguousarray(scaled.reshape(k // 512, 128, 4, n).transpose(0, 1, 3, 2))
    if fmt == "e4m3":
        words = by_word.astype(ml_dtypes.float8_e4m3fn).view(np.uint8)
    else:
        c = by_word.astype(ml_dtypes.float4_e2m1fn).view(np.uint8) & 0xF
        words = (c[..., 0::2] | (c[..., 1::2] << 4)).reshape(k // 512, 128, 2 * n)
    return np.ascontiguousarray(words), np.ascontiguousarray(byte.astype(np.uint8).reshape(k // 512, 16, n))


def unpack_weight(words, scales, fmt):
    g, _, n = scales.shape
    words = np.ascontiguousarray(words).reshape(g, 128, n, -1)
    if fmt == "e4m3":
        vals = words.view(ml_dtypes.float8_e4m3fn).astype(np.float64)
    else:
        nib = np.empty((g, 128, n, 4), np.uint8)
        nib[..., 0::2] = words & 0xF
        nib[..., 1::2] = words >> 4
        vals = E2M1[nib]
    vals = vals * np.repeat(np.exp2(scales.astype(np.float64) - 127.0), 8, axis=1)[..., None]
    return vals.transpose(0, 1, 3, 2).reshape(g * 512, n)


D, T, U, I, Q = 512, 1024, 1024, 512, 128


def setup_inputs():
    n = np.random.standard_normal
    idx = np.stack([np.random.permutation(T)[:I] for _ in range(8)])
    idx2 = np.stack([np.random.permutation(U)[:I] for _ in range(8)])
    idx3 = np.stack([np.random.permutation(U)[:I] for _ in range(8)])
    idx4 = np.stack([np.random.permutation(T)[:I] for _ in range(8)])
    fd = mx_kscale(D)
    cachep = pack_weight(n((D, T)) / fd[:, None], "e4m3")
    draftp = pack_weight(n((D, U)) / fd[:, None], "e2m1")
    return {
        "query": (n((D, Q)) * 1.0 / np.sqrt(D) * fd[:, None]).astype(np.float32),
        "cache_words": cachep[0],
        "cache_scales": cachep[1],
        "draft_words": draftp[0],
        "draft_scales": draftp[1],
        "offs": striped8(idx),
        "offs2": striped8(idx2),
        "offs3": striped8(idx3),
        "offs4": striped8(idx4),
    }


def reference(query, cache_words, cache_scales, draft_words, draft_scales, offs, offs2, offs3, offs4):
    idx = unstriped8(offs)
    idx2 = unstriped8(offs2)
    idx3 = unstriped8(offs3)
    idx4 = unstriped8(offs4)
    cacheu = unpack_weight(cache_words, cache_scales, "e4m3")
    draftu = unpack_weight(draft_words, draft_scales, "e2m1")
    queryq = mxq(f64(query), 0, "e4m3")
    a = queryq.T @ cacheu
    b = queryq.T @ draftu
    a1 = np.pad(a, ((0, 0), (1, 0)))[:, :T]
    dl = a - a1
    f1 = np.zeros((Q, U))
    f1[np.arange(Q)[:, None], idx2[np.arange(Q) % 128 // 16]] = pick8(dl, idx, 16)
    bb = b + f1
    v = np.maximum(pick8(bb, idx3, 16), pick8(dl, idx4, 16))
    f2 = np.zeros((Q, T))
    f2[np.arange(Q)[:, None], idx[np.arange(Q) % 128 // 16]] = v
    aa = a - f2
    y = pick8(aa, idx4, 16)
    return y

@@ -1,0 +1,147 @@
+from contextlib import ExitStack
+
+import concourse.mybir as mybir
+
+F32 = mybir.dt.float32
+BF16 = mybir.dt.bfloat16
+I32 = mybir.dt.int32
+U32 = mybir.dt.uint32
+U16 = mybir.dt.uint16
+U8 = mybir.dt.uint8
+FP8X4 = mybir.dt.float8_e4m3fn_x4
+FP4X4 = mybir.dt.float4_e2m1fn_x4
+COPY = mybir.ActivationFunctionType.Copy
+ADD = mybir.AluOpType.add
+SUB = mybir.AluOpType.subtract
+MAX = mybir.AluOpType.max
+
+P = 128
+D, T, U, I, Q = 512, 1024, 1024, 512, 128
+FLOPS = 2 * D * Q * (T + U)
+PACK = 4
+HALF = I // 2
+PAD = 8
+A_N = 256
+B_N = 512
+
+
+def tile_attend_slopes_two_kernel(tc, query, cache_words, cache_scales, draft_words, draft_scales, offs, offs2, offs3, offs4, out):
+    nc = tc.nc
+    with ExitStack() as ctx:
+        lists = ctx.enter_context(tc.tile_pool(name="lists", bufs=1))
+        keep = ctx.enter_context(tc.tile_pool(name="keep", bufs=1))
+        psum = ctx.enter_context(tc.psum_pool(name="psum", bufs=1))
+
+        idx = lists.tile([P, I // 16], U16, name="idx")
+        idx2 = lists.tile([P, I // 16], U16, name="idx2")
+        idx3 = lists.tile([P, I // 16], U16, name="idx3")
+        idx4 = lists.tile([P, I // 16], U16, name="idx4")
+
+        c_plane = keep.tile([P, T], U8, name="c_plane", align_bytes=64)
+        d_plane = keep.tile([P, U], U8, name="d_plane", align_bytes=64)
+        f1 = keep.tile([P, U], F32, name="f1")
+        f2 = keep.tile([P, T], F32, name="f2")
+        a_pad = keep.tile([P, PAD + T], F32, name="a_pad")
+        nc.vector.memset(c_plane[:].bitcast(I32), 0)
+        nc.vector.memset(d_plane[:].bitcast(I32), 0)
+        nc.vector.memset(a_pad[:, PAD - 1 : PAD], 0.0)
+        nc.vector.memset(f1[:], 0.0)
+        nc.vector.memset(f2[:], 0.0)
+
+        q_raw = keep.tile([P, PACK, Q], F32, name="q_raw")
+        nc.sync.dma_start(out=q_raw[:], in_=query.rearrange("(p j) q -> p j q", j=PACK))
+        for quad in range(4):
+            nc.scalar.dma_start(
+                out=c_plane[32 * quad : 32 * quad + 4, :].bitcast(I32),
+                in_=cache_scales[0, 4 * quad : 4 * quad + 4, :].bitcast(I32),
+            )
+        c_src = cache_words[0].rearrange("p n t -> p (n t)").bitcast(I32)
+        c_words = []
+        for h in range(2):
+            w = keep.tile([P, T // 2], I32, name="c_words%d" % h, align_bytes=64)
+            nc.sync.dma_start(out=w[:], in_=c_src[:, h * (T // 2) : (h + 1) * (T // 2)])
+            c_words.append(w)
+        nc.sync.dma_start(idx[:], offs)
+        nc.sync.dma_start(idx2[:], offs2)
+        nc.sync.dma_start(idx4[:], offs4)
+        d_words = keep.tile([P, 2 * U], U8, name="d_words", align_bytes=64)
+        nc.sync.dma_start(out=d_words[:].bitcast(I32), in_=draft_words[0].bitcast(I32))
+        nc.sync.dma_start(idx3[:], offs3)
+        for quad in range(4):
+            nc.gpsimd.dma_start(
+                out=d_plane[32 * quad : 32 * quad + 4, :].bitcast(I32),
+                in_=draft_scales[0, 4 * quad : 4 * quad + 4, :].bitcast(I32),
+            )
+
+        q_bf = keep.tile([P, Q, PACK], BF16, name="q_bf", align_bytes=64)
+        nc.vector.tensor_copy(
+            out=q_bf[:].rearrange("p (c i) t -> p c t i", i=4),
+            in_=q_raw[:].rearrange("p t (c i) -> p c t i", i=4),
+        )
+        q_codes = keep.tile([P, Q], U32, name="q_codes", align_bytes=64)
+        q_plane = keep.tile([P, Q], U8, name="q_plane", align_bytes=64)
+        nc.vector.quantize_mx(out=q_codes[:].bitcast(FP8X4), scales=q_plane[:], in_=q_bf[:].rearrange("p q t -> p (q t)"))
+
+        dl = keep.tile([P, T], F32, name="dl")
+        a_banks = []
+        for j in range(T // A_N):
+            bank = psum.tile([P, A_N], F32, name="a_bank%d" % j)
+            h, c0 = divmod(j * A_N, T // 2)
+            nc.tensor.matmul_mx(
+                out=bank[:],
+                lhsT=q_codes[:].bitcast(FP8X4),
+                lhsT_scale=q_plane[:],
+                rhs=c_words[h][:, c0 : c0 + A_N].bitcast(FP8X4),
+                rhs_scale=c_plane[:, j * A_N : (j + 1) * A_N],
+                start=True,
+                stop=True,
+            )
+            nc.scalar.activation(a_pad[:, PAD + j * A_N : PAD + (j + 1) * A_N], bank[:], COPY)
+            nc.vector.tensor_tensor(
+                dl[:, j * A_N : (j + 1) * A_N], bank[:], a_pad[:, PAD - 1 + j * A_N : PAD - 1 + (j + 1) * A_N], SUB
+            )
+            a_banks.append(bank)
+        b_banks = []
+        for j in range(U // B_N):
+            bank = psum.tile([P, B_N], F32, name="b_bank%d" % j)
+            nc.tensor.matmul_mx(
+                out=bank[:],
+                lhsT=q_codes[:].bitcast(FP8X4),
+                lhsT_scale=q_plane[:],
+                rhs=d_words[:, 2 * j * B_N : 2 * (j + 1) * B_N].bitcast(FP4X4),
+                rhs_scale=d_plane[:, j * B_N : (j + 1) * B_N],
+                start=True,
+                stop=True,
+            )
+            b_banks.append(bank)
+
+        halves = [(slice(h * HALF, (h + 1) * HALF), slice(h * HALF // 16, (h + 1) * HALF // 16)) for h in range(2)]
+
+        g1 = keep.tile([P, I], F32, name="g1")
+        for slots, cols in halves:
+            nc.vector.tensor_copy(g1[:, slots], dl[:].indirect(idx[:, cols]))
+            nc.scalar.activation(f1[:].indirect(idx2[:, cols]), g1[:, slots], COPY)
+        g4 = keep.tile([P, I], F32, name="g4")
+        nc.vector.tensor_copy(g4[:], dl[:].indirect(idx4[:]))
+
+        bb = keep.tile([P, U], F32, name="bb")
+        for j in range(U // B_N):
+            cols = slice(j * B_N, (j + 1) * B_N)
+            nc.vector.tensor_tensor(bb[:, cols], b_banks[j][:], f1[:, cols], ADD)
+
+        g3 = keep.tile([P, I], F32, name="g3")
+        v = keep.tile([P, I], F32, name="v")
+        for slots, cols in halves:
+            nc.vector.tensor_copy(g3[:, slots], bb[:].indirect(idx3[:, cols]))
+            nc.vector.tensor_tensor(v[:, slots], g3[:, slots], g4[:, slots], MAX)
+            nc.scalar.activation(f2[:].indirect(idx[:, cols]), v[:, slots], COPY)
+
+        aa = keep.tile([P, T], F32, name="aa")
+        nc.vector.tensor_tensor(aa[:], a_pad[:, PAD:], f2[:], SUB)
+
+        y0 = keep.tile([P, HALF], F32, name="y0")
+        y1 = keep.tile([P, HALF], F32, name="y1")
+        nc.vector.tensor_copy(y0[:], aa[:].indirect(idx4[:, halves[0][1]]))
+        nc.sync.dma_start(out=out[:, halves[0][0]], in_=y0[:])
+        nc.scalar.activation(y1[:], aa[:].indirect(idx4[:, halves[1][1]]), COPY)
+        nc.scalar.dma_start(out=out[:, halves[1][0]], in_=y1[:])

@@ -21,8 +21,10 @@ FLOPS = 2 * D * Q * (T + U)
 PACK = 4
 HALF = I // 2
 PAD = 8
-A_N = 256
+A_CUTS = (0, 128, 384, 640, 896, 1024)
+C_SPLIT = 384
 B_N = 512
+LEAD = 128
 
 
 def tile_attend_slopes_two_kernel(tc, query, cache_words, cache_scales, draft_words, draft_scales, offs, offs2, offs3, offs4, out):
@@ -40,66 +42,68 @@ def tile_attend_slopes_two_kernel(tc, query, cache_words, cache_scales, draft_wo
         c_plane = keep.tile([P, T], U8, name="c_plane", align_bytes=64)
         d_plane = keep.tile([P, U], U8, name="d_plane", align_bytes=64)
         f1 = keep.tile([P, U], F32, name="f1")
-        f2 = keep.tile([P, T], F32, name="f2")
         a_pad = keep.tile([P, PAD + T], F32, name="a_pad")
-        nc.vector.memset(c_plane[:].bitcast(I32), 0)
-        nc.vector.memset(d_plane[:].bitcast(I32), 0)
+        nc.gpsimd.memset(c_plane[:].bitcast(I32), 0)
+        nc.gpsimd.memset(d_plane[:].bitcast(I32), 0)
         nc.vector.memset(a_pad[:, PAD - 1 : PAD], 0.0)
         nc.vector.memset(f1[:], 0.0)
-        nc.vector.memset(f2[:], 0.0)
 
         q_raw = keep.tile([P, PACK, Q], F32, name="q_raw")
         nc.sync.dma_start(out=q_raw[:], in_=query.rearrange("(p j) q -> p j q", j=PACK))
+        c_src = cache_words[0].rearrange("p n t -> p (n t)").bitcast(I32)
+        c_words = [keep.tile([P, n], I32, name="c_words%d" % n, align_bytes=64) for n in (C_SPLIT, T - C_SPLIT)]
+        nc.sync.dma_start(out=c_words[0][:], in_=c_src[:, :C_SPLIT])
         for quad in range(4):
-            nc.scalar.dma_start(
+            nc.sync.dma_start(
                 out=c_plane[32 * quad : 32 * quad + 4, :].bitcast(I32),
                 in_=cache_scales[0, 4 * quad : 4 * quad + 4, :].bitcast(I32),
             )
-        c_src = cache_words[0].rearrange("p n t -> p (n t)").bitcast(I32)
-        c_words = []
-        for h in range(2):
-            w = keep.tile([P, T // 2], I32, name="c_words%d" % h, align_bytes=64)
-            nc.sync.dma_start(out=w[:], in_=c_src[:, h * (T // 2) : (h + 1) * (T // 2)])
-            c_words.append(w)
+        nc.sync.dma_start(out=c_words[1][:], in_=c_src[:, C_SPLIT:])
         nc.sync.dma_start(idx[:], offs)
         nc.sync.dma_start(idx2[:], offs2)
         nc.sync.dma_start(idx4[:], offs4)
         d_words = keep.tile([P, 2 * U], U8, name="d_words", align_bytes=64)
         nc.sync.dma_start(out=d_words[:].bitcast(I32), in_=draft_words[0].bitcast(I32))
-        nc.sync.dma_start(idx3[:], offs3)
         for quad in range(4):
-            nc.gpsimd.dma_start(
+            nc.sync.dma_start(
                 out=d_plane[32 * quad : 32 * quad + 4, :].bitcast(I32),
                 in_=draft_scales[0, 4 * quad : 4 * quad + 4, :].bitcast(I32),
             )
+        nc.sync.dma_start(idx3[:], offs3)
 
-        q_bf = keep.tile([P, Q, PACK], BF16, name="q_bf", align_bytes=64)
-        nc.vector.tensor_copy(
-            out=q_bf[:].rearrange("p (c i) t -> p c t i", i=4),
-            in_=q_raw[:].rearrange("p t (c i) -> p c t i", i=4),
-        )
         q_codes = keep.tile([P, Q], U32, name="q_codes", align_bytes=64)
         q_plane = keep.tile([P, Q], U8, name="q_plane", align_bytes=64)
-        nc.vector.quantize_mx(out=q_codes[:].bitcast(FP8X4), scales=q_plane[:], in_=q_bf[:].rearrange("p q t -> p (q t)"))
+        q_bf = [keep.tile([P, Q // 2, PACK], BF16, name="q_bf%d" % h, tag="q_bf%d" % h, align_bytes=64) for h in range(2)]
+        for h in range(2):
+            nc.vector.tensor_copy(
+                out=q_bf[h][:].rearrange("p (c i) t -> p c t i", i=4),
+                in_=q_raw[:, :, h * Q // 2 : (h + 1) * Q // 2].rearrange("p t (c i) -> p c t i", i=4),
+            )
+        for h in range(2):
+            rows = slice(h * Q // 2, (h + 1) * Q // 2)
+            nc.vector.quantize_mx(
+                out=q_codes[:, rows].bitcast(FP8X4), scales=q_plane[:, rows], in_=q_bf[h][:].rearrange("p q t -> p (q t)")
+            )
+
+        f2 = keep.tile([P, T], F32, name="f2", tag="q_bf1", align_bytes=64)
+        nc.vector.memset(f2[:], 0.0)
 
         dl = keep.tile([P, T], F32, name="dl")
         a_banks = []
-        for j in range(T // A_N):
-            bank = psum.tile([P, A_N], F32, name="a_bank%d" % j)
-            h, c0 = divmod(j * A_N, T // 2)
+        for lo, hi in zip(A_CUTS[:-1], A_CUTS[1:]):
+            bank = psum.tile([P, hi - lo], F32, name="a_bank%d" % lo)
+            h, c0 = divmod(lo, C_SPLIT) if lo < C_SPLIT else (1, lo - C_SPLIT)
             nc.tensor.matmul_mx(
                 out=bank[:],
                 lhsT=q_codes[:].bitcast(FP8X4),
                 lhsT_scale=q_plane[:],
-                rhs=c_words[h][:, c0 : c0 + A_N].bitcast(FP8X4),
-                rhs_scale=c_plane[:, j * A_N : (j + 1) * A_N],
+                rhs=c_words[h][:, c0 : c0 + hi - lo].bitcast(FP8X4),
+                rhs_scale=c_plane[:, lo:hi],
                 start=True,
                 stop=True,
             )
-            nc.scalar.activation(a_pad[:, PAD + j * A_N : PAD + (j + 1) * A_N], bank[:], COPY)
-            nc.vector.tensor_tensor(
-                dl[:, j * A_N : (j + 1) * A_N], bank[:], a_pad[:, PAD - 1 + j * A_N : PAD - 1 + (j + 1) * A_N], SUB
-            )
+            nc.scalar.activation(a_pad[:, PAD + lo : PAD + hi], bank[:], COPY)
+            nc.vector.tensor_tensor(dl[:, lo:hi], bank[:], a_pad[:, PAD - 1 + lo : PAD - 1 + hi], SUB)
             a_banks.append(bank)
         b_banks = []
         for j in range(U // B_N):
@@ -131,10 +135,11 @@ def tile_attend_slopes_two_kernel(tc, query, cache_words, cache_scales, draft_wo
 
         g3 = keep.tile([P, I], F32, name="g3")
         v = keep.tile([P, I], F32, name="v")
-        for slots, cols in halves:
-            nc.vector.tensor_copy(g3[:, slots], bb[:].indirect(idx3[:, cols]))
-            nc.vector.tensor_tensor(v[:, slots], g3[:, slots], g4[:, slots], MAX)
-            nc.scalar.activation(f2[:].indirect(idx[:, cols]), v[:, slots], COPY)
+        nc.vector.tensor_copy(g3[:, halves[0][0]], bb[:].indirect(idx3[:, halves[0][1]]))
+        nc.scalar.activation(g3[:, halves[1][0]], bb[:].indirect(idx3[:, halves[1][1]]), COPY)
+        for lo, hi in ((0, LEAD), (LEAD, I)):
+            nc.vector.tensor_tensor(v[:, lo:hi], g3[:, lo:hi], g4[:, lo:hi], MAX)
+            nc.scalar.activation(f2[:].indirect(idx[:, lo // 16 : hi // 16]), v[:, lo:hi], COPY)
 
         aa = keep.tile([P, T], F32, name="aa")
         nc.vector.tensor_tensor(aa[:], a_pad[:, PAD:], f2[:], SUB)

@@ -24,7 +24,7 @@ PAD = 8
 A_CUTS = (0, 128, 384, 640, 896, 1024)
 C_SPLIT = 384
 B_N = 512
-LEAD = 128
+LEAD = 96
 
 
 def tile_attend_slopes_two_kernel(tc, query, cache_words, cache_scales, draft_words, draft_scales, offs, offs2, offs3, offs4, out):
@@ -41,12 +41,13 @@ def tile_attend_slopes_two_kernel(tc, query, cache_words, cache_scales, draft_wo
 
         c_plane = keep.tile([P, T], U8, name="c_plane", align_bytes=64)
         d_plane = keep.tile([P, U], U8, name="d_plane", align_bytes=64)
-        f1 = keep.tile([P, U], F32, name="f1")
+        f1 = [keep.tile([P, U], F32, name="f1_%d" % h) for h in range(2)]
         a_pad = keep.tile([P, PAD + T], F32, name="a_pad")
         nc.gpsimd.memset(c_plane[:].bitcast(I32), 0)
-        nc.gpsimd.memset(d_plane[:].bitcast(I32), 0)
+        nc.vector.memset(d_plane[:].bitcast(I32), 0)
         nc.vector.memset(a_pad[:, PAD - 1 : PAD], 0.0)
-        nc.vector.memset(f1[:], 0.0)
+        for window in f1:
+            nc.vector.memset(window[:], 0.0)
 
         q_raw = keep.tile([P, PACK, Q], F32, name="q_raw")
         nc.sync.dma_start(out=q_raw[:], in_=query.rearrange("(p j) q -> p j q", j=PACK))
@@ -62,7 +63,7 @@ def tile_attend_slopes_two_kernel(tc, query, cache_words, cache_scales, draft_wo
         nc.sync.dma_start(idx[:], offs)
         nc.sync.dma_start(idx2[:], offs2)
         nc.sync.dma_start(idx4[:], offs4)
-        d_words = keep.tile([P, 2 * U], U8, name="d_words", align_bytes=64)
+        d_words = keep.tile([P, 2 * U], U8, name="d_words", tag="d_words", align_bytes=64)
         nc.sync.dma_start(out=d_words[:].bitcast(I32), in_=draft_words[0].bitcast(I32))
         for quad in range(4):
             nc.sync.dma_start(
@@ -85,8 +86,8 @@ def tile_attend_slopes_two_kernel(tc, query, cache_words, cache_scales, draft_wo
                 out=q_codes[:, rows].bitcast(FP8X4), scales=q_plane[:, rows], in_=q_bf[h][:].rearrange("p q t -> p (q t)")
             )
 
-        f2 = keep.tile([P, T], F32, name="f2", tag="q_bf1", align_bytes=64)
-        nc.vector.memset(f2[:], 0.0)
+        f2_lead = keep.tile([P, T], F32, name="f2_lead", tag="q_bf1", align_bytes=64)
+        nc.vector.memset(f2_lead[:], 0.0)
 
         dl = keep.tile([P, T], F32, name="dl")
         a_banks = []
@@ -119,30 +120,37 @@ def tile_attend_slopes_two_kernel(tc, query, cache_words, cache_scales, draft_wo
             )
             b_banks.append(bank)
 
+        f2_rest = keep.tile([P, T], F32, name="f2_rest", tag="d_words", align_bytes=64)
+        nc.gpsimd.memset(f2_rest[:], 0.0)
+
         halves = [(slice(h * HALF, (h + 1) * HALF), slice(h * HALF // 16, (h + 1) * HALF // 16)) for h in range(2)]
 
         g1 = keep.tile([P, I], F32, name="g1")
-        for slots, cols in halves:
+        for window, (slots, cols) in zip(f1, halves):
             nc.vector.tensor_copy(g1[:, slots], dl[:].indirect(idx[:, cols]))
-            nc.scalar.activation(f1[:].indirect(idx2[:, cols]), g1[:, slots], COPY)
+            nc.scalar.activation(window[:].indirect(idx2[:, cols]), g1[:, slots], COPY)
         g4 = keep.tile([P, I], F32, name="g4")
         nc.vector.tensor_copy(g4[:], dl[:].indirect(idx4[:]))
 
+        b_part = keep.tile([P, U], F32, name="b_part")
         bb = keep.tile([P, U], F32, name="bb")
         for j in range(U // B_N):
             cols = slice(j * B_N, (j + 1) * B_N)
-            nc.vector.tensor_tensor(bb[:, cols], b_banks[j][:], f1[:, cols], ADD)
+            nc.vector.tensor_tensor(b_part[:, cols], b_banks[j][:], f1[0][:, cols], ADD)
+        nc.vector.tensor_tensor(bb[:], b_part[:], f1[1][:], ADD)
 
         g3 = keep.tile([P, I], F32, name="g3")
         v = keep.tile([P, I], F32, name="v")
         nc.vector.tensor_copy(g3[:, halves[0][0]], bb[:].indirect(idx3[:, halves[0][1]]))
         nc.scalar.activation(g3[:, halves[1][0]], bb[:].indirect(idx3[:, halves[1][1]]), COPY)
-        for lo, hi in ((0, LEAD), (LEAD, I)):
+        for window, lo, hi in ((f2_lead, 0, LEAD), (f2_rest, LEAD, I)):
             nc.vector.tensor_tensor(v[:, lo:hi], g3[:, lo:hi], g4[:, lo:hi], MAX)
-            nc.scalar.activation(f2[:].indirect(idx[:, lo // 16 : hi // 16]), v[:, lo:hi], COPY)
+            nc.scalar.activation(window[:].indirect(idx[:, lo // 16 : hi // 16]), v[:, lo:hi], COPY)
 
         aa = keep.tile([P, T], F32, name="aa")
-        nc.vector.tensor_tensor(aa[:], a_pad[:, PAD:], f2[:], SUB)
+        a_part = keep.tile([P, T], F32, name="a_part")
+        nc.vector.tensor_tensor(a_part[:], a_pad[:, PAD:], f2_lead[:], SUB)
+        nc.vector.tensor_tensor(aa[:], a_part[:], f2_rest[:], SUB)
 
         y0 = keep.tile([P, HALF], F32, name="y0")
         y1 = keep.tile([P, HALF], F32, name="y1")

@@ -15,106 +15,114 @@ ADD = mybir.AluOpType.add
 SUB = mybir.AluOpType.subtract
 MAX = mybir.AluOpType.max
 
-P = 128
 D, T, U, I, Q = 512, 1024, 1024, 512, 128
 FLOPS = 2 * D * Q * (T + U)
+
+P = 128
 PACK = 4
+QUADRANTS = 4
+HEAD = 16
 HALF = I // 2
 PAD = 8
+BANK = 512
 A_CUTS = (0, 128, 384, 640, 896, 1024)
-C_SPLIT = 384
-B_N = 512
+C_SPLIT = A_CUTS[2]
 LEAD = 96
 
 
-def tile_attend_slopes_two_kernel(tc, query, cache_words, cache_scales, draft_words, draft_scales, offs, offs2, offs3, offs4, out):
+def list_cols(lo, hi):
+    return slice(lo // HEAD, hi // HEAD)
+
+
+def load_plane(nc, plane, scales):
+    for quad in range(QUADRANTS):
+        nc.sync.dma_start(
+            out=plane[32 * quad : 32 * quad + 4, :].bitcast(I32),
+            in_=scales[0, 4 * quad : 4 * quad + 4, :].bitcast(I32),
+        )
+
+
+def tile_attend_slopes_two_kernel(
+    tc, query, cache_words, cache_scales, draft_words, draft_scales, offs, offs2, offs3, offs4, out
+):
     nc = tc.nc
     with ExitStack() as ctx:
         lists = ctx.enter_context(tc.tile_pool(name="lists", bufs=1))
         keep = ctx.enter_context(tc.tile_pool(name="keep", bufs=1))
         psum = ctx.enter_context(tc.psum_pool(name="psum", bufs=1))
 
-        idx = lists.tile([P, I // 16], U16, name="idx")
-        idx2 = lists.tile([P, I // 16], U16, name="idx2")
-        idx3 = lists.tile([P, I // 16], U16, name="idx3")
-        idx4 = lists.tile([P, I // 16], U16, name="idx4")
+        idx = lists.tile([P, I // HEAD], U16, name="idx")
+        idx2 = lists.tile([P, I // HEAD], U16, name="idx2")
+        idx3 = lists.tile([P, I // HEAD], U16, name="idx3")
+        idx4 = lists.tile([P, I // HEAD], U16, name="idx4")
 
         c_plane = keep.tile([P, T], U8, name="c_plane", align_bytes=64)
         d_plane = keep.tile([P, U], U8, name="d_plane", align_bytes=64)
         f1 = [keep.tile([P, U], F32, name="f1_%d" % h) for h in range(2)]
         a_pad = keep.tile([P, PAD + T], F32, name="a_pad")
-        nc.gpsimd.memset(c_plane[:].bitcast(I32), 0)
-        nc.vector.memset(d_plane[:].bitcast(I32), 0)
         nc.vector.memset(a_pad[:, PAD - 1 : PAD], 0.0)
         for window in f1:
             nc.vector.memset(window[:], 0.0)
 
         q_raw = keep.tile([P, PACK, Q], F32, name="q_raw")
-        nc.sync.dma_start(out=q_raw[:], in_=query.rearrange("(p j) q -> p j q", j=PACK))
-        c_src = cache_words[0].rearrange("p n t -> p (n t)").bitcast(I32)
+        nc.sync.dma_start(out=q_raw[:], in_=query.rearrange("(p r) q -> p r q", r=PACK))
+        c_src = cache_words[0].rearrange("p n r -> p (n r)").bitcast(I32)
         c_words = [keep.tile([P, n], I32, name="c_words%d" % n, align_bytes=64) for n in (C_SPLIT, T - C_SPLIT)]
         nc.sync.dma_start(out=c_words[0][:], in_=c_src[:, :C_SPLIT])
-        for quad in range(4):
-            nc.sync.dma_start(
-                out=c_plane[32 * quad : 32 * quad + 4, :].bitcast(I32),
-                in_=cache_scales[0, 4 * quad : 4 * quad + 4, :].bitcast(I32),
-            )
+        load_plane(nc, c_plane, cache_scales)
         nc.sync.dma_start(out=c_words[1][:], in_=c_src[:, C_SPLIT:])
         nc.sync.dma_start(idx[:], offs)
         nc.sync.dma_start(idx2[:], offs2)
         nc.sync.dma_start(idx4[:], offs4)
         d_words = keep.tile([P, 2 * U], U8, name="d_words", tag="d_words", align_bytes=64)
         nc.sync.dma_start(out=d_words[:].bitcast(I32), in_=draft_words[0].bitcast(I32))
-        for quad in range(4):
-            nc.sync.dma_start(
-                out=d_plane[32 * quad : 32 * quad + 4, :].bitcast(I32),
-                in_=draft_scales[0, 4 * quad : 4 * quad + 4, :].bitcast(I32),
-            )
+        load_plane(nc, d_plane, draft_scales)
         nc.sync.dma_start(idx3[:], offs3)
 
         q_codes = keep.tile([P, Q], U32, name="q_codes", align_bytes=64)
         q_plane = keep.tile([P, Q], U8, name="q_plane", align_bytes=64)
         q_bf = [keep.tile([P, Q // 2, PACK], BF16, name="q_bf%d" % h, tag="q_bf%d" % h, align_bytes=64) for h in range(2)]
-        for h in range(2):
+        q_halves = [slice(h * Q // 2, (h + 1) * Q // 2) for h in range(2)]
+        for rounded, rows in zip(q_bf, q_halves):
             nc.vector.tensor_copy(
-                out=q_bf[h][:].rearrange("p (c i) t -> p c t i", i=4),
-                in_=q_raw[:, :, h * Q // 2 : (h + 1) * Q // 2].rearrange("p t (c i) -> p c t i", i=4),
+                out=rounded[:].rearrange("p (c i) r -> p c r i", i=4),
+                in_=q_raw[:, :, rows].rearrange("p r (c i) -> p c r i", i=4),
             )
-        for h in range(2):
-            rows = slice(h * Q // 2, (h + 1) * Q // 2)
+        for rounded, rows in zip(q_bf, q_halves):
             nc.vector.quantize_mx(
-                out=q_codes[:, rows].bitcast(FP8X4), scales=q_plane[:, rows], in_=q_bf[h][:].rearrange("p q t -> p (q t)")
+                out=q_codes[:, rows].bitcast(FP8X4),
+                scales=q_plane[:, rows],
+                in_=rounded[:].rearrange("p q r -> p (q r)"),
             )
 
         f2_lead = keep.tile([P, T], F32, name="f2_lead", tag="q_bf1", align_bytes=64)
         nc.vector.memset(f2_lead[:], 0.0)
 
         dl = keep.tile([P, T], F32, name="dl")
-        a_banks = []
         for lo, hi in zip(A_CUTS[:-1], A_CUTS[1:]):
             bank = psum.tile([P, hi - lo], F32, name="a_bank%d" % lo)
-            h, c0 = divmod(lo, C_SPLIT) if lo < C_SPLIT else (1, lo - C_SPLIT)
+            words = c_words[0][:, lo:hi] if lo < C_SPLIT else c_words[1][:, lo - C_SPLIT : hi - C_SPLIT]
             nc.tensor.matmul_mx(
                 out=bank[:],
                 lhsT=q_codes[:].bitcast(FP8X4),
                 lhsT_scale=q_plane[:],
-                rhs=c_words[h][:, c0 : c0 + hi - lo].bitcast(FP8X4),
+                rhs=words.bitcast(FP8X4),
                 rhs_scale=c_plane[:, lo:hi],
                 start=True,
                 stop=True,
             )
             nc.scalar.activation(a_pad[:, PAD + lo : PAD + hi], bank[:], COPY)
             nc.vector.tensor_tensor(dl[:, lo:hi], bank[:], a_pad[:, PAD - 1 + lo : PAD - 1 + hi], SUB)
-            a_banks.append(bank)
+
         b_banks = []
-        for j in range(U // B_N):
-            bank = psum.tile([P, B_N], F32, name="b_bank%d" % j)
+        for lo in range(0, U, BANK):
+            bank = psum.tile([P, BANK], F32, name="b_bank%d" % lo)
             nc.tensor.matmul_mx(
                 out=bank[:],
                 lhsT=q_codes[:].bitcast(FP8X4),
                 lhsT_scale=q_plane[:],
-                rhs=d_words[:, 2 * j * B_N : 2 * (j + 1) * B_N].bitcast(FP4X4),
-                rhs_scale=d_plane[:, j * B_N : (j + 1) * B_N],
+                rhs=d_words[:, 2 * lo : 2 * (lo + BANK)].bitcast(FP4X4),
+                rhs_scale=d_plane[:, lo : lo + BANK],
                 start=True,
                 stop=True,
             )
@@ -123,38 +131,36 @@ def tile_attend_slopes_two_kernel(tc, query, cache_words, cache_scales, draft_wo
         f2_rest = keep.tile([P, T], F32, name="f2_rest", tag="d_words", align_bytes=64)
         nc.gpsimd.memset(f2_rest[:], 0.0)
 
-        halves = [(slice(h * HALF, (h + 1) * HALF), slice(h * HALF // 16, (h + 1) * HALF // 16)) for h in range(2)]
-
-        g1 = keep.tile([P, I], F32, name="g1")
-        for window, (slots, cols) in zip(f1, halves):
-            nc.vector.tensor_copy(g1[:, slots], dl[:].indirect(idx[:, cols]))
-            nc.scalar.activation(window[:].indirect(idx2[:, cols]), g1[:, slots], COPY)
-        g4 = keep.tile([P, I], F32, name="g4")
-        nc.vector.tensor_copy(g4[:], dl[:].indirect(idx4[:]))
+        dl_by_idx = keep.tile([P, I], F32, name="dl_by_idx")
+        for window, lo in zip(f1, (0, HALF)):
+            cols = list_cols(lo, lo + HALF)
+            nc.vector.tensor_copy(dl_by_idx[:, lo : lo + HALF], dl[:].indirect(idx[:, cols]))
+            nc.scalar.activation(window[:].indirect(idx2[:, cols]), dl_by_idx[:, lo : lo + HALF], COPY)
+        dl_by_idx4 = keep.tile([P, I], F32, name="dl_by_idx4")
+        nc.vector.tensor_copy(dl_by_idx4[:], dl[:].indirect(idx4[:]))
 
         b_part = keep.tile([P, U], F32, name="b_part")
         bb = keep.tile([P, U], F32, name="bb")
-        for j in range(U // B_N):
-            cols = slice(j * B_N, (j + 1) * B_N)
-            nc.vector.tensor_tensor(b_part[:, cols], b_banks[j][:], f1[0][:, cols], ADD)
+        for bank, lo in zip(b_banks, range(0, U, BANK)):
+            nc.vector.tensor_tensor(b_part[:, lo : lo + BANK], bank[:], f1[0][:, lo : lo + BANK], ADD)
         nc.vector.tensor_tensor(bb[:], b_part[:], f1[1][:], ADD)
 
-        g3 = keep.tile([P, I], F32, name="g3")
+        bb_by_idx3 = keep.tile([P, I], F32, name="bb_by_idx3")
         v = keep.tile([P, I], F32, name="v")
-        nc.vector.tensor_copy(g3[:, halves[0][0]], bb[:].indirect(idx3[:, halves[0][1]]))
-        nc.scalar.activation(g3[:, halves[1][0]], bb[:].indirect(idx3[:, halves[1][1]]), COPY)
+        nc.vector.tensor_copy(bb_by_idx3[:, :HALF], bb[:].indirect(idx3[:, list_cols(0, HALF)]))
+        nc.scalar.activation(bb_by_idx3[:, HALF:], bb[:].indirect(idx3[:, list_cols(HALF, I)]), COPY)
         for window, lo, hi in ((f2_lead, 0, LEAD), (f2_rest, LEAD, I)):
-            nc.vector.tensor_tensor(v[:, lo:hi], g3[:, lo:hi], g4[:, lo:hi], MAX)
-            nc.scalar.activation(window[:].indirect(idx[:, lo // 16 : hi // 16]), v[:, lo:hi], COPY)
+            nc.vector.tensor_tensor(v[:, lo:hi], bb_by_idx3[:, lo:hi], dl_by_idx4[:, lo:hi], MAX)
+            nc.scalar.activation(window[:].indirect(idx[:, list_cols(lo, hi)]), v[:, lo:hi], COPY)
 
         aa = keep.tile([P, T], F32, name="aa")
         a_part = keep.tile([P, T], F32, name="a_part")
         nc.vector.tensor_tensor(a_part[:], a_pad[:, PAD:], f2_lead[:], SUB)
         nc.vector.tensor_tensor(aa[:], a_part[:], f2_rest[:], SUB)
 
-        y0 = keep.tile([P, HALF], F32, name="y0")
-        y1 = keep.tile([P, HALF], F32, name="y1")
-        nc.vector.tensor_copy(y0[:], aa[:].indirect(idx4[:, halves[0][1]]))
-        nc.sync.dma_start(out=out[:, halves[0][0]], in_=y0[:])
-        nc.scalar.activation(y1[:], aa[:].indirect(idx4[:, halves[1][1]]), COPY)
-        nc.scalar.dma_start(out=out[:, halves[1][0]], in_=y1[:])
+        out_lo = keep.tile([P, HALF], F32, name="out_lo")
+        out_hi = keep.tile([P, HALF], F32, name="out_hi")
+        nc.vector.tensor_copy(out_lo[:], aa[:].indirect(idx4[:, list_cols(0, HALF)]))
+        nc.sync.dma_start(out=out[:, :HALF], in_=out_lo[:])
+        nc.scalar.activation(out_hi[:], aa[:].indirect(idx4[:, list_cols(HALF, I)]), COPY)
+        nc.scalar.dma_start(out=out[:, HALF:], in_=out_hi[:])

from contextlib import ExitStack

import concourse.mybir as mybir

F32 = mybir.dt.float32
BF16 = mybir.dt.bfloat16
I32 = mybir.dt.int32
U32 = mybir.dt.uint32
U16 = mybir.dt.uint16
U8 = mybir.dt.uint8
FP8X4 = mybir.dt.float8_e4m3fn_x4
FP4X4 = mybir.dt.float4_e2m1fn_x4
COPY = mybir.ActivationFunctionType.Copy
ADD = mybir.AluOpType.add
SUB = mybir.AluOpType.subtract
MAX = mybir.AluOpType.max

D, T, U, I, Q = 512, 1024, 1024, 512, 128
FLOPS = 2 * D * Q * (T + U)

P = 128
PACK = 4
QUADRANTS = 4
HEAD = 16
HALF = I // 2
PAD = 8
BANK = 512
A_CUTS = (0, 128, 384, 640, 896, 1024)
C_SPLIT = A_CUTS[2]
LEAD = 96


def list_cols(lo, hi):
    return slice(lo // HEAD, hi // HEAD)


def load_plane(nc, plane, scales):
    for quad in range(QUADRANTS):
        nc.sync.dma_start(
            out=plane[32 * quad : 32 * quad + 4, :].bitcast(I32),
            in_=scales[0, 4 * quad : 4 * quad + 4, :].bitcast(I32),
        )


def tile_attend_slopes_two_kernel(
    tc, query, cache_words, cache_scales, draft_words, draft_scales, offs, offs2, offs3, offs4, out
):
    nc = tc.nc
    with ExitStack() as ctx:
        lists = ctx.enter_context(tc.tile_pool(name="lists", bufs=1))
        keep = ctx.enter_context(tc.tile_pool(name="keep", bufs=1))
        psum = ctx.enter_context(tc.psum_pool(name="psum", bufs=1))

        idx = lists.tile([P, I // HEAD], U16, name="idx")
        idx2 = lists.tile([P, I // HEAD], U16, name="idx2")
        idx3 = lists.tile([P, I // HEAD], U16, name="idx3")
        idx4 = lists.tile([P, I // HEAD], U16, name="idx4")

        c_plane = keep.tile([P, T], U8, name="c_plane", align_bytes=64)
        d_plane = keep.tile([P, U], U8, name="d_plane", align_bytes=64)
        f1 = [keep.tile([P, U], F32, name="f1_%d" % h) for h in range(2)]
        a_pad = keep.tile([P, PAD + T], F32, name="a_pad")
        nc.vector.memset(a_pad[:, PAD - 1 : PAD], 0.0)
        for window in f1:
            nc.vector.memset(window[:], 0.0)

        q_raw = keep.tile([P, PACK, Q], F32, name="q_raw")
        nc.sync.dma_start(out=q_raw[:], in_=query.rearrange("(p r) q -> p r q", r=PACK))
        c_src = cache_words[0].rearrange("p n r -> p (n r)").bitcast(I32)
        c_words = [keep.tile([P, n], I32, name="c_words%d" % n, align_bytes=64) for n in (C_SPLIT, T - C_SPLIT)]
        nc.sync.dma_start(out=c_words[0][:], in_=c_src[:, :C_SPLIT])
        load_plane(nc, c_plane, cache_scales)
        nc.sync.dma_start(out=c_words[1][:], in_=c_src[:, C_SPLIT:])
        nc.sync.dma_start(idx[:], offs)
        nc.sync.dma_start(idx2[:], offs2)
        nc.sync.dma_start(idx4[:], offs4)
        d_words = keep.tile([P, 2 * U], U8, name="d_words", tag="d_words", align_bytes=64)
        nc.sync.dma_start(out=d_words[:].bitcast(I32), in_=draft_words[0].bitcast(I32))
        load_plane(nc, d_plane, draft_scales)
        nc.sync.dma_start(idx3[:], offs3)

        q_codes = keep.tile([P, Q], U32, name="q_codes", align_bytes=64)
        q_plane = keep.tile([P, Q], U8, name="q_plane", align_bytes=64)
        q_bf = [keep.tile([P, Q // 2, PACK], BF16, name="q_bf%d" % h, tag="q_bf%d" % h, align_bytes=64) for h in range(2)]
        q_halves = [slice(h * Q // 2, (h + 1) * Q // 2) for h in range(2)]
        for rounded, rows in zip(q_bf, q_halves):
            nc.vector.tensor_copy(
                out=rounded[:].rearrange("p (c i) r -> p c r i", i=4),
                in_=q_raw[:, :, rows].rearrange("p r (c i) -> p c r i", i=4),
            )
        for rounded, rows in zip(q_bf, q_halves):
            nc.vector.quantize_mx(
                out=q_codes[:, rows].bitcast(FP8X4),
                scales=q_plane[:, rows],
                in_=rounded[:].rearrange("p q r -> p (q r)"),
            )

        f2_lead = keep.tile([P, T], F32, name="f2_lead", tag="q_bf1", align_bytes=64)
        nc.vector.memset(f2_lead[:], 0.0)

        dl = keep.tile([P, T], F32, name="dl")
        for lo, hi in zip(A_CUTS[:-1], A_CUTS[1:]):
            bank = psum.tile([P, hi - lo], F32, name="a_bank%d" % lo)
            words = c_words[0][:, lo:hi] if lo < C_SPLIT else c_words[1][:, lo - C_SPLIT : hi - C_SPLIT]
            nc.tensor.matmul_mx(
                out=bank[:],
                lhsT=q_codes[:].bitcast(FP8X4),
                lhsT_scale=q_plane[:],
                rhs=words.bitcast(FP8X4),
                rhs_scale=c_plane[:, lo:hi],
                start=True,
                stop=True,
            )
            nc.scalar.activation(a_pad[:, PAD + lo : PAD + hi], bank[:], COPY)
            nc.vector.tensor_tensor(dl[:, lo:hi], bank[:], a_pad[:, PAD - 1 + lo : PAD - 1 + hi], SUB)

        b_banks = []
        for lo in range(0, U, BANK):
            bank = psum.tile([P, BANK], F32, name="b_bank%d" % lo)
            nc.tensor.matmul_mx(
                out=bank[:],
                lhsT=q_codes[:].bitcast(FP8X4),
                lhsT_scale=q_plane[:],
                rhs=d_words[:, 2 * lo : 2 * (lo + BANK)].bitcast(FP4X4),
                rhs_scale=d_plane[:, lo : lo + BANK],
                start=True,
                stop=True,
            )
            b_banks.append(bank)

        f2_rest = keep.tile([P, T], F32, name="f2_rest", tag="d_words", align_bytes=64)
        nc.gpsimd.memset(f2_rest[:], 0.0)

        dl_by_idx = keep.tile([P, I], F32, name="dl_by_idx")
        for window, lo in zip(f1, (0, HALF)):
            cols = list_cols(lo, lo + HALF)
            nc.vector.tensor_copy(dl_by_idx[:, lo : lo + HALF], dl[:].indirect(idx[:, cols]))
            nc.scalar.activation(window[:].indirect(idx2[:, cols]), dl_by_idx[:, lo : lo + HALF], COPY)
        dl_by_idx4 = keep.tile([P, I], F32, name="dl_by_idx4")
        nc.vector.tensor_copy(dl_by_idx4[:], dl[:].indirect(idx4[:]))

        b_part = keep.tile([P, U], F32, name="b_part")
        bb = keep.tile([P, U], F32, name="bb")
        for bank, lo in zip(b_banks, range(0, U, BANK)):
            nc.vector.tensor_tensor(b_part[:, lo : lo + BANK], bank[:], f1[0][:, lo : lo + BANK], ADD)
        nc.vector.tensor_tensor(bb[:], b_part[:], f1[1][:], ADD)

        bb_by_idx3 = keep.tile([P, I], F32, name="bb_by_idx3")
        v = keep.tile([P, I], F32, name="v")
        nc.vector.tensor_copy(bb_by_idx3[:, :HALF], bb[:].indirect(idx3[:, list_cols(0, HALF)]))
        nc.scalar.activation(bb_by_idx3[:, HALF:], bb[:].indirect(idx3[:, list_cols(HALF, I)]), COPY)
        for window, lo, hi in ((f2_lead, 0, LEAD), (f2_rest, LEAD, I)):
            nc.vector.tensor_tensor(v[:, lo:hi], bb_by_idx3[:, lo:hi], dl_by_idx4[:, lo:hi], MAX)
            nc.scalar.activation(window[:].indirect(idx[:, list_cols(lo, hi)]), v[:, lo:hi], COPY)

        aa = keep.tile([P, T], F32, name="aa")
        a_part = keep.tile([P, T], F32, name="a_part")
        nc.vector.tensor_tensor(a_part[:], a_pad[:, PAD:], f2_lead[:], SUB)
        nc.vector.tensor_tensor(aa[:], a_part[:], f2_rest[:], SUB)

        out_lo = keep.tile([P, HALF], F32, name="out_lo")
        out_hi = keep.tile([P, HALF], F32, name="out_hi")
        nc.vector.tensor_copy(out_lo[:], aa[:].indirect(idx4[:, list_cols(0, HALF)]))
        nc.sync.dma_start(out=out[:, :HALF], in_=out_lo[:])
        nc.scalar.activation(out_hi[:], aa[:].indirect(idx4[:, list_cols(HALF, I)]), COPY)
        nc.scalar.dma_start(out=out[:, HALF:], in_=out_hi[:])
